import numpy as np
import ml_dtypes


def mxq(x, axis, fmt="e4m3"):
    dtype, down = {"e4m3": (ml_dtypes.float8_e4m3fn, 7), "e5m2": (ml_dtypes.float8_e5m2, 14)}[fmt]
    v = np.moveaxis(np.asarray(x, np.float32).astype(ml_dtypes.bfloat16).astype(np.float64), axis, -1)
    blocks = v.reshape(v.shape[:-1] + (-1, 32))
    amax = np.abs(blocks).max(-1, keepdims=True)
    byte = np.maximum(np.where(amax > 0, np.frexp(amax)[1] - 1 + 127, 0) - down, 1)
    scale = np.exp2(byte - 127.0)
    codes = (blocks / scale).astype(np.float32).astype(dtype).astype(np.float64)
    return np.moveaxis((codes * scale).reshape(v.shape), -1, axis)


WIDE = False


def mx_kscale(k):
    if not WIDE:
        return np.ones(k)
    levels = np.array([30, -30])
    if k % 512:
        return np.exp2(np.random.permutation(np.resize(levels, k // 32))).repeat(32)
    a = np.empty((k // 512, 16))
    for p in range(k // 512):
        a[p, :8] = np.random.permutation(np.resize(levels, 8))
        for g in range(8):
            far = levels[np.abs(levels - a[p, g]) >= 10]
            a[p, g + 8] = far[np.random.randint(len(far))]
    return np.exp2(a.ravel()).repeat(32)


def f64(x):
    return np.asarray(x).astype(np.float64)


def striped(idx):
    return np.tile(np.asarray(idx).reshape(-1, 16).T, (8, 1)).astype(np.uint16)


def unstriped(offs):
    return offs[:16].T.reshape(-1).astype(np.int64)


E2M1 = np.array([0.0, 0.5, 1.0, 1.5, 2.0, 3.0, 4.0, 6.0, -0.0, -0.5, -1.0, -1.5, -2.0, -3.0, -4.0, -6.0])


def pack_weight(w, fmt):
    k, n = w.shape
    w = f64(np.asarray(w, np.float32).astype(ml_dtypes.bfloat16)).reshape(k // 32, 32, n)
    amax = np.abs(w).max(1)
    if fmt in ("e4m3", "e5m2"):
        byte = np.frexp(amax)[1] - 1 + 127 - (7 if fmt == "e4m3" else 14)
    else:
        mant, ex = np.frexp(amax / 6.0)
        byte = np.where(mant > 0.5, ex, ex - 1) + 127
    byte = np.clip(np.where(amax > 0, byte, 1), 1, 254)
    scaled = (w * np.exp2(127.0 - byte)[:, None, :]).reshape(k, n).astype(np.float32)
    by_word = np.ascontiguousarray(scaled.reshape(k // 512, 128, 4, n).transpose(0, 1, 3, 2))
    if fmt in ("e4m3", "e5m2"):
        words = by_word.astype(ml_dtypes.float8_e4m3fn if fmt == "e4m3" else ml_dtypes.float8_e5m2).view(np.uint8)
    else:
        c = by_word.astype(ml_dtypes.float4_e2m1fn).view(np.uint8) & 0xF
        words = (c[..., 0::2] | (c[..., 1::2] << 4)).reshape(k // 512, 128, 2 * n)
    return np.ascontiguousarray(words), np.ascontiguousarray(byte.astype(np.uint8).reshape(k // 512, 16, n))


def unpack_weight(words, scales, fmt):
    g, _, n = scales.shape
    words = np.ascontiguousarray(words).reshape(g, 128, n, -1)
    if fmt in ("e4m3", "e5m2"):
        vals = words.view(ml_dtypes.float8_e4m3fn if fmt == "e4m3" else ml_dtypes.float8_e5m2).astype(np.float64)
    else:
        nib = np.empty((g, 128, n, 4), np.uint8)
        nib[..., 0::2] = words & 0xF
        nib[..., 1::2] = words >> 4
        vals = E2M1[nib]
    vals = vals * np.repeat(np.exp2(scales.astype(np.float64) - 127.0), 8, axis=1)[..., None]
    return vals.transpose(0, 1, 3, 2).reshape(g * 512, n)


def sgn(shape):
    return np.random.uniform(0.5, 2.0, shape) * np.where(np.random.standard_normal(shape) < 0, -1.0, 1.0)


K, F, T, Z, J, R, O, N = 512, 512, 1024, 1024, 256, 512, 128, 256


def setup_inputs():
    n = np.random.standard_normal
    idx = np.random.permutation(T)[:J]
    idx2 = np.random.permutation(Z)[:J]
    idx3 = np.random.permutation(J)[:O]
    idx4 = np.random.permutation(J)[:O]
    idx5 = np.random.permutation(J)[:O]
    idx6 = np.random.permutation(T)[:O]
    fk = mx_kscale(K)
    fr = mx_kscale(R)
    ff = mx_kscale(F)
    xtp = pack_weight(n((K, T)) / fk[:, None], "e2m1")
    wp = pack_weight(n((K, R)) * 1 / np.sqrt(K) * fk[:, None] * fr, "e5m2")
    xop = pack_weight(n((F, Z)) / ff[:, None], "e5m2")
    w0p = pack_weight(n((F, R)) * 1 / np.sqrt(F) * ff[:, None] * fr, "e4m3")
    wbp = pack_weight(n((R, N)) * 1 / np.sqrt(R) / fr[:, None], "e4m3")
    wsp = pack_weight(n((K, N)) * 1 / np.sqrt(K) * fk[:, None], "e4m3")
    return {
        "xt_words": xtp[0],
        "xt_scales": xtp[1],
        "w_words": wp[0],
        "w_scales": wp[1],
        "xo_words": xop[0],
        "xo_scales": xop[1],
        "w0_words": w0p[0],
        "w0_scales": w0p[1],
        "sa": (sgn((R, 1))).astype(np.float32),
        "sb": (sgn((R, 1))).astype(np.float32),
        "sd": (sgn((R, 1))).astype(np.float32),
        "wb_words": wbp[0],
        "wb_scales": wbp[1],
        "ws_words": wsp[0],
        "ws_scales": wsp[1],
        "offs": striped(idx),
        "offs2": striped(idx2),
        "offs3": striped(idx3),
        "offs4": striped(idx4),
        "offs5": striped(idx5),
        "offs6": striped(idx6),
    }


def reference(xt_words, xt_scales, w_words, w_scales, xo_words, xo_scales, w0_words, w0_scales, sa, sb, sd, wb_words, wb_scales, ws_words, ws_scales, offs, offs2, offs3, offs4, offs5, offs6):
    idx = unstriped(offs)
    idx2 = unstriped(offs2)
    idx3 = unstriped(offs3)
    idx4 = unstriped(offs4)
    idx5 = unstriped(offs5)
    idx6 = unstriped(offs6)
    xtu = unpack_weight(xt_words, xt_scales, "e2m1")
    wu = unpack_weight(w_words, w_scales, "e5m2")
    xou = unpack_weight(xo_words, xo_scales, "e5m2")
    w0u = unpack_weight(w0_words, w0_scales, "e4m3")
    wbu = unpack_weight(wb_words, wb_scales, "e4m3")
    wsu = unpack_weight(ws_words, ws_scales, "e4m3")
    xtidxg = xtu[:, idx]
    xoidx2g = xou[:, idx2]
    a = wu.T @ xtidxg + w0u.T @ xoidx2g
    hid = np.maximum(a[:, idx3] * f64(sa) + a[:, idx4] * f64(sb) + a[:, idx5] * f64(sd), 0.0)
    hidq = mxq(hid, 0, "e5m2")
    xtidx6g = xtu[:, idx6]
    y = wbu.T @ hidq + wsu.T @ xtidx6g
    return y

@@ -1,0 +1,174 @@
+from contextlib import ExitStack
+
+import concourse.mybir as mybir
+
+F32 = mybir.dt.float32
+BF16 = mybir.dt.bfloat16
+I32 = mybir.dt.int32
+U32 = mybir.dt.uint32
+U16 = mybir.dt.uint16
+U8 = mybir.dt.uint8
+E4M3 = mybir.dt.float8_e4m3fn_x4
+E5M2 = mybir.dt.float8_e5m2_x4
+E2M1 = mybir.dt.float4_e2m1fn_x4
+ALU = mybir.AluOpType
+ACT = mybir.ActivationFunctionType
+
+P = 128
+T, J, R, O, N = 1024, 256, 512, 128, 256
+FLOPS = 335544320
+
+
+def tile_list_tripleblend_bank_further_plain_kernel(
+    tc, xt_words, xt_scales, w_words, w_scales, xo_words, xo_scales, w0_words, w0_scales,
+    sa, sb, sd, wb_words, wb_scales, ws_words, ws_scales,
+    offs, offs2, offs3, offs4, offs5, offs6, out,
+):
+    nc = tc.nc
+    with ExitStack() as ctx:
+        lists = ctx.enter_context(tc.tile_pool(name="lists", bufs=1))
+        keep = ctx.enter_context(tc.tile_pool(name="keep", bufs=1))
+        psum = ctx.enter_context(tc.psum_pool(name="psum", bufs=1))
+
+        def sb_tile(name, shape, dtype, tag=None):
+            return keep.tile(shape, dtype, name=name, tag=tag or name, align_bytes=64)
+
+        l1 = lists.tile([P, J // 16], U16, name="l1")
+        l2 = lists.tile([P, J // 16], U16, name="l2")
+        l3 = lists.tile([P, O // 16], U16, name="l3")
+        l4 = lists.tile([P, O // 16], U16, name="l4")
+        l5 = lists.tile([P, O // 16], U16, name="l5")
+        l6 = lists.tile([P, O // 16], U16, name="l6")
+
+        xt_w = sb_tile("xt_w", [P, T], U16)
+        xo_w = sb_tile("xo_w", [P, T], U32)
+        w_raw = sb_tile("w_raw", [P, R], U32)
+        w0_raw = sb_tile("w0_raw", [P, R], U32)
+        wb_w = sb_tile("wb_w", [P, N], U32)
+        ws_w = sb_tile("ws_w", [P, N], U32)
+        xt_s = sb_tile("xt_s", [P, T], U8)
+        xo_s = sb_tile("xo_s", [P, T], U8)
+        ww_s = sb_tile("ww_s", [P, 2 * R], U8)
+        wo_s = sb_tile("wo_s", [P, 2 * N], U8)
+        sa_t = sb_tile("sa_t", [P, 4], F32)
+        sb_t = sb_tile("sb_t", [P, 4], F32)
+        sd_t = sb_tile("sd_t", [P, 4], F32)
+
+        def words(dram):
+            return dram[0].rearrange("p n t -> p (n t)").bitcast(I32)
+
+        ww_s_st = sb_tile("ww_s_st", [4, 4, 256], I32)
+        nc.vector.memset(ww_s[:].bitcast(I32), 0)
+        xt_s_st = sb_tile("xt_s_st", [4, 4, 256], I32)
+        nc.vector.memset(xt_s[:].bitcast(I32), 0)
+
+        nc.sync.dma_start(ww_s_st[:, :, 0:128], w_scales[0].bitcast(I32).rearrange("(q r) c -> r q c", r=4))
+        nc.sync.dma_start(ww_s_st[:, :, 128:256], w0_scales[0].bitcast(I32).rearrange("(q r) c -> r q c", r=4))
+        nc.sync.dma_start(l1[:], offs)
+        nc.sync.dma_start(xt_s_st[:, :, 0:256], xt_scales[0].bitcast(I32).rearrange("(q r) c -> r q c", r=4))
+        nc.sync.dma_start(xt_w[:].bitcast(I32), xt_words[0].bitcast(I32))
+        nc.sync.dma_start(w_raw[:].bitcast(I32), words(w_words))
+        nc.sync.dma_start(w0_raw[:].bitcast(I32), words(w0_words))
+        nc.sync.dma_start(xo_w[:].bitcast(I32), words(xo_words))
+        nc.gpsimd.dma_start(sa_t[:], sa.rearrange("(p t) o -> p (t o)", t=4))
+        nc.gpsimd.dma_start(sb_t[:], sb.rearrange("(p t) o -> p (t o)", t=4))
+        nc.gpsimd.dma_start(sd_t[:], sd.rearrange("(p t) o -> p (t o)", t=4))
+        nc.sync.dma_start(l2[:], offs2)
+        nc.sync.dma_start(xo_s[0:32, :].bitcast(I32)[:, 0:256], xo_scales[0].bitcast(I32)[0:4, :].unsqueeze(0).to_broadcast([8, 4, 256]))
+        nc.sync.dma_start(xo_s[32:64, :].bitcast(I32)[:, 0:256], xo_scales[0].bitcast(I32)[4:8, :].unsqueeze(0).to_broadcast([8, 4, 256]))
+        nc.sync.dma_start(xo_s[64:96, :].bitcast(I32)[:, 0:256], xo_scales[0].bitcast(I32)[8:12, :].unsqueeze(0).to_broadcast([8, 4, 256]))
+        nc.sync.dma_start(xo_s[96:128, :].bitcast(I32)[:, 0:256], xo_scales[0].bitcast(I32)[12:16, :].unsqueeze(0).to_broadcast([8, 4, 256]))
+        nc.sync.dma_start(l3[:], offs3)
+        nc.sync.dma_start(l4[:], offs4)
+        nc.sync.dma_start(l5[:], offs5)
+        nc.sync.dma_start(l6[:], offs6)
+        nc.sync.dma_start(ws_w[:].bitcast(I32), words(ws_words))
+        nc.sync.dma_start(wb_w[:].bitcast(I32), words(wb_words))
+        nc.sync.dma_start(wo_s[0:32, :].bitcast(I32)[:, 64:128], ws_scales[0].bitcast(I32)[0:4, :].unsqueeze(0).to_broadcast([8, 4, 64]))
+        nc.sync.dma_start(wo_s[32:64, :].bitcast(I32)[:, 64:128], ws_scales[0].bitcast(I32)[4:8, :].unsqueeze(0).to_broadcast([8, 4, 64]))
+        nc.sync.dma_start(wo_s[64:96, :].bitcast(I32)[:, 64:128], ws_scales[0].bitcast(I32)[8:12, :].unsqueeze(0).to_broadcast([8, 4, 64]))
+        nc.sync.dma_start(wo_s[96:128, :].bitcast(I32)[:, 64:128], ws_scales[0].bitcast(I32)[12:16, :].unsqueeze(0).to_broadcast([8, 4, 64]))
+        nc.sync.dma_start(wo_s[0:32, :].bitcast(I32)[:, 0:64], wb_scales[0].bitcast(I32)[0:4, :].unsqueeze(0).to_broadcast([8, 4, 64]))
+        nc.sync.dma_start(wo_s[32:64, :].bitcast(I32)[:, 0:64], wb_scales[0].bitcast(I32)[4:8, :].unsqueeze(0).to_broadcast([8, 4, 64]))
+        nc.sync.dma_start(wo_s[64:96, :].bitcast(I32)[:, 0:64], wb_scales[0].bitcast(I32)[8:12, :].unsqueeze(0).to_broadcast([8, 4, 64]))
+        nc.sync.dma_start(wo_s[96:128, :].bitcast(I32)[:, 0:64], wb_scales[0].bitcast(I32)[12:16, :].unsqueeze(0).to_broadcast([8, 4, 64]))
+
+        w_p = sb_tile("w_p", [P, R], U32)
+        w0_p = sb_tile("w0_p", [P, R], U32)
+        ww_sp = sb_tile("ww_sp", [P, 2 * R], U8)
+        xt_g = sb_tile("xt_g", [P, J], U16)
+        xt_sg = sb_tile("xt_sg", [P, J], U8)
+        xo_g = sb_tile("xo_g", [P, J], U32)
+        xo_sg = sb_tile("xo_sg", [P, J], U8)
+        x6_g = sb_tile("x6_g", [P, O], U16, "xo_s")
+        x6_sg = sb_tile("x6_sg", [P, O], U8, "xo_g")
+
+        for q in range(4):
+            nc.vector.tensor_copy(ww_s[32 * q:32 * q + 4, :].bitcast(I32), ww_s_st[:, q, :])
+        nc.vector.tensor_copy(ww_sp[:].rearrange("p (a t m) -> p a t m", a=2, t=4), ww_s[:].rearrange("p (a m t) -> p a t m", a=2, t=4))
+        for q in range(4):
+            nc.vector.tensor_copy(xt_s[32 * q:32 * q + 4, :].bitcast(I32), xt_s_st[:, q, :])
+        nc.vector.tensor_copy(xt_g[:], xt_w[:].indirect(l1[:]))
+        nc.vector.tensor_copy(xt_sg[:], xt_s[:].indirect(l1[:]))
+        nc.vector.tensor_copy(xo_g[:], xo_w[:].indirect(l2[:]))
+        nc.vector.tensor_copy(xo_sg[:], xo_s[:].indirect(l2[:]))
+
+        nc.scalar.copy(w_p[:].rearrange("p (t m) -> p m t", t=4), w_raw[:].rearrange("p (m t) -> p m t", t=4))
+        nc.scalar.copy(w0_p[:].rearrange("p (t m) -> p m t", t=4), w0_raw[:].rearrange("p (m t) -> p m t", t=4))
+
+        a_ps = [psum.tile([P, J], F32, name="a_ps%d" % t) for t in range(4)]
+        for t in range(4):
+            c = slice(P * t, P * t + P)
+            nc.tensor.matmul_mx(out=a_ps[t][:], lhsT=w_p[:, c].bitcast(E5M2), lhsT_scale=ww_sp[:, c],
+                                rhs=xt_g[:].bitcast(E2M1), rhs_scale=xt_sg[:], start=True, stop=False)
+        for t in range(4):
+            c = slice(P * t, P * t + P)
+            nc.tensor.matmul_mx(out=a_ps[t][:], lhsT=w0_p[:, c].bitcast(E4M3), lhsT_scale=ww_sp[:, R + P * t:R + P * t + P],
+                                rhs=xo_g[:].bitcast(E5M2), rhs_scale=xo_sg[:], start=False, stop=True)
+
+        a_sb = [sb_tile("a_sb%d" % t, [P, J], F32) for t in range(4)]
+        for t in range(4):
+            nc.vector.tensor_copy(a_sb[t][:], a_ps[t][:])
+
+        nc.vector.tensor_copy(x6_g[:], xt_w[:].indirect(l6[:]))
+        nc.vector.tensor_copy(x6_sg[:], xt_s[:].indirect(l6[:]))
+        y_ps = [psum.tile([P, O], F32, name="y_ps%d" % h) for h in range(2)]
+        for h in range(2):
+            nc.tensor.matmul_mx(out=y_ps[h][:], lhsT=ws_w[:, P * h:P * h + P].bitcast(E4M3), lhsT_scale=wo_s[:, N + P * h:N + P * h + P],
+                                rhs=x6_g[:].bitcast(E2M1), rhs_scale=x6_sg[:], start=True, stop=False)
+
+        ga = sb_tile("ga", [P, 4, O], F32)
+        gb = sb_tile("gb", [P, 4, O], F32)
+        gd = sb_tile("gd", [P, 4, O], F32)
+        s2 = sb_tile("s2", [P, 4, O], F32, "xt_w")
+        s3 = sb_tile("s3", [P, 4, O], F32, "xt_s")
+        hb = sb_tile("hb", [P, O, 4], BF16)
+        hq = sb_tile("hq", [P, O], U32)
+        hs = sb_tile("hs", [P, O], U8)
+
+        def blend(t, lo, hi):
+            c = slice(lo, hi)
+            k = slice(lo // 16, hi // 16)
+            nc.scalar.activation(ga[:, t, c], a_sb[t][:].indirect(l3[:, k]), ACT.Copy, scale=sa_t[:, t:t + 1])
+            nc.scalar.activation(gb[:, t, c], a_sb[t][:].indirect(l4[:, k]), ACT.Copy, scale=sb_t[:, t:t + 1])
+            nc.vector.tensor_tensor(s2[:, t, c], ga[:, t, c], gb[:, t, c], ALU.add)
+            nc.scalar.activation(gd[:, t, c], a_sb[t][:].indirect(l5[:, k]), ACT.Copy, scale=sd_t[:, t:t + 1])
+            nc.vector.tensor_tensor(s3[:, t, c], s2[:, t, c], gd[:, t, c], ALU.add)
+
+        for t in range(3):
+            blend(t, 0, O)
+        for lo in (0, O // 2):
+            hi = lo + O // 2
+            blend(3, lo, hi)
+            nc.vector.tensor_scalar(hb[:, lo:hi, :], s3[:, :, lo:hi].rearrange("p t o -> p o t"), 0.0, None, ALU.max)
+            nc.vector.quantize_mx(out=hq[:, lo:hi].bitcast(E5M2), scales=hs[:, lo:hi], in_=hb[:, lo:hi, :].rearrange("p o t -> p (o t)"))
+
+        for h in range(2):
+            nc.tensor.matmul_mx(out=y_ps[h][:], lhsT=wb_w[:, P * h:P * h + P].bitcast(E4M3), lhsT_scale=wo_s[:, P * h:P * h + P],
+                                rhs=hq[:].bitcast(E5M2), rhs_scale=hs[:], start=False, stop=True)
+        y0 = sb_tile("y0", [P, O], F32)
+        y1 = sb_tile("y1", [P, O], F32)
+        nc.vector.tensor_copy(y0[:], y_ps[0][:])
+        nc.scalar.copy(y1[:], y_ps[1][:])
+        nc.sync.dma_start(out[0:P, :], y0[:])
+        nc.scalar.dma_start(out[P:2 * P, :], y1[:])

@@ -57,41 +57,45 @@ def tile_list_tripleblend_bank_further_plain_kernel(
         def words(dram):
             return dram[0].rearrange("p n t -> p (n t)").bitcast(I32)
 
+        nc.vector.memset(xt_s[:].bitcast(I32), 0)
+        nc.vector.memset(xo_s[:].bitcast(I32), 0)
         ww_s_st = sb_tile("ww_s_st", [4, 4, 256], I32)
         nc.vector.memset(ww_s[:].bitcast(I32), 0)
-        xt_s_st = sb_tile("xt_s_st", [4, 4, 256], I32)
-        nc.vector.memset(xt_s[:].bitcast(I32), 0)
+        nc.vector.memset(wo_s[:].bitcast(I32), 0)
 
         nc.sync.dma_start(ww_s_st[:, :, 0:128], w_scales[0].bitcast(I32).rearrange("(q r) c -> r q c", r=4))
         nc.sync.dma_start(ww_s_st[:, :, 128:256], w0_scales[0].bitcast(I32).rearrange("(q r) c -> r q c", r=4))
         nc.sync.dma_start(l1[:], offs)
-        nc.sync.dma_start(xt_s_st[:, :, 0:256], xt_scales[0].bitcast(I32).rearrange("(q r) c -> r q c", r=4))
         nc.sync.dma_start(xt_w[:].bitcast(I32), xt_words[0].bitcast(I32))
+        nc.sync.dma_start(xt_s[0:4, :].bitcast(I32)[:, 0:256], xt_scales[0].bitcast(I32)[0:4, :])
+        nc.sync.dma_start(xt_s[32:36, :].bitcast(I32)[:, 0:256], xt_scales[0].bitcast(I32)[4:8, :])
         nc.sync.dma_start(w_raw[:].bitcast(I32), words(w_words))
-        nc.sync.dma_start(w0_raw[:].bitcast(I32), words(w0_words))
         nc.sync.dma_start(xo_w[:].bitcast(I32), words(xo_words))
         nc.gpsimd.dma_start(sa_t[:], sa.rearrange("(p t) o -> p (t o)", t=4))
         nc.gpsimd.dma_start(sb_t[:], sb.rearrange("(p t) o -> p (t o)", t=4))
         nc.gpsimd.dma_start(sd_t[:], sd.rearrange("(p t) o -> p (t o)", t=4))
+        nc.sync.dma_start(xt_s[64:68, :].bitcast(I32)[:, 0:256], xt_scales[0].bitcast(I32)[8:12, :])
+        nc.sync.dma_start(xt_s[96:100, :].bitcast(I32)[:, 0:256], xt_scales[0].bitcast(I32)[12:16, :])
         nc.sync.dma_start(l2[:], offs2)
-        nc.sync.dma_start(xo_s[0:32, :].bitcast(I32)[:, 0:256], xo_scales[0].bitcast(I32)[0:4, :].unsqueeze(0).to_broadcast([8, 4, 256]))
-        nc.sync.dma_start(xo_s[32:64, :].bitcast(I32)[:, 0:256], xo_scales[0].bitcast(I32)[4:8, :].unsqueeze(0).to_broadcast([8, 4, 256]))
-        nc.sync.dma_start(xo_s[64:96, :].bitcast(I32)[:, 0:256], xo_scales[0].bitcast(I32)[8:12, :].unsqueeze(0).to_broadcast([8, 4, 256]))
-        nc.sync.dma_start(xo_s[96:128, :].bitcast(I32)[:, 0:256], xo_scales[0].bitcast(I32)[12:16, :].unsqueeze(0).to_broadcast([8, 4, 256]))
+        nc.sync.dma_start(w0_raw[:].bitcast(I32), words(w0_words))
+        nc.sync.dma_start(xo_s[0:4, :].bitcast(I32)[:, 0:256], xo_scales[0].bitcast(I32)[0:4, :])
+        nc.sync.dma_start(xo_s[32:36, :].bitcast(I32)[:, 0:256], xo_scales[0].bitcast(I32)[4:8, :])
+        nc.sync.dma_start(xo_s[64:68, :].bitcast(I32)[:, 0:256], xo_scales[0].bitcast(I32)[8:12, :])
+        nc.sync.dma_start(xo_s[96:100, :].bitcast(I32)[:, 0:256], xo_scales[0].bitcast(I32)[12:16, :])
         nc.sync.dma_start(l3[:], offs3)
         nc.sync.dma_start(l4[:], offs4)
         nc.sync.dma_start(l5[:], offs5)
         nc.sync.dma_start(l6[:], offs6)
         nc.sync.dma_start(ws_w[:].bitcast(I32), words(ws_words))
         nc.sync.dma_start(wb_w[:].bitcast(I32), words(wb_words))
-        nc.sync.dma_start(wo_s[0:32, :].bitcast(I32)[:, 64:128], ws_scales[0].bitcast(I32)[0:4, :].unsqueeze(0).to_broadcast([8, 4, 64]))
-        nc.sync.dma_start(wo_s[32:64, :].bitcast(I32)[:, 64:128], ws_scales[0].bitcast(I32)[4:8, :].unsqueeze(0).to_broadcast([8, 4, 64]))
-        nc.sync.dma_start(wo_s[64:96, :].bitcast(I32)[:, 64:128], ws_scales[0].bitcast(I32)[8:12, :].unsqueeze(0).to_broadcast([8, 4, 64]))
-        nc.sync.dma_start(wo_s[96:128, :].bitcast(I32)[:, 64:128], ws_scales[0].bitcast(I32)[12:16, :].unsqueeze(0).to_broadcast([8, 4, 64]))
-        nc.sync.dma_start(wo_s[0:32, :].bitcast(I32)[:, 0:64], wb_scales[0].bitcast(I32)[0:4, :].unsqueeze(0).to_broadcast([8, 4, 64]))
-        nc.sync.dma_start(wo_s[32:64, :].bitcast(I32)[:, 0:64], wb_scales[0].bitcast(I32)[4:8, :].unsqueeze(0).to_broadcast([8, 4, 64]))
-        nc.sync.dma_start(wo_s[64:96, :].bitcast(I32)[:, 0:64], wb_scales[0].bitcast(I32)[8:12, :].unsqueeze(0).to_broadcast([8, 4, 64]))
-        nc.sync.dma_start(wo_s[96:128, :].bitcast(I32)[:, 0:64], wb_scales[0].bitcast(I32)[12:16, :].unsqueeze(0).to_broadcast([8, 4, 64]))
+        nc.sync.dma_start(wo_s[0:4, :].bitcast(I32)[:, 64:128], ws_scales[0].bitcast(I32)[0:4, :])
+        nc.sync.dma_start(wo_s[32:36, :].bitcast(I32)[:, 64:128], ws_scales[0].bitcast(I32)[4:8, :])
+        nc.sync.dma_start(wo_s[64:68, :].bitcast(I32)[:, 64:128], ws_scales[0].bitcast(I32)[8:12, :])
+        nc.sync.dma_start(wo_s[96:100, :].bitcast(I32)[:, 64:128], ws_scales[0].bitcast(I32)[12:16, :])
+        nc.sync.dma_start(wo_s[0:4, :].bitcast(I32)[:, 0:64], wb_scales[0].bitcast(I32)[0:4, :])
+        nc.sync.dma_start(wo_s[32:36, :].bitcast(I32)[:, 0:64], wb_scales[0].bitcast(I32)[4:8, :])
+        nc.sync.dma_start(wo_s[64:68, :].bitcast(I32)[:, 0:64], wb_scales[0].bitcast(I32)[8:12, :])
+        nc.sync.dma_start(wo_s[96:100, :].bitcast(I32)[:, 0:64], wb_scales[0].bitcast(I32)[12:16, :])
 
         w_p = sb_tile("w_p", [P, R], U32)
         w0_p = sb_tile("w0_p", [P, R], U32)
@@ -106,29 +110,32 @@ def tile_list_tripleblend_bank_further_plain_kernel(
         for q in range(4):
             nc.vector.tensor_copy(ww_s[32 * q:32 * q + 4, :].bitcast(I32), ww_s_st[:, q, :])
         nc.vector.tensor_copy(ww_sp[:].rearrange("p (a t m) -> p a t m", a=2, t=4), ww_s[:].rearrange("p (a m t) -> p a t m", a=2, t=4))
-        for q in range(4):
-            nc.vector.tensor_copy(xt_s[32 * q:32 * q + 4, :].bitcast(I32), xt_s_st[:, q, :])
         nc.vector.tensor_copy(xt_g[:], xt_w[:].indirect(l1[:]))
         nc.vector.tensor_copy(xt_sg[:], xt_s[:].indirect(l1[:]))
         nc.vector.tensor_copy(xo_g[:], xo_w[:].indirect(l2[:]))
-        nc.vector.tensor_copy(xo_sg[:], xo_s[:].indirect(l2[:]))
+        for u in range(2):
+            nc.vector.tensor_copy(xo_sg[:, P * u:P * u + P], xo_s[:].indirect(l2[:, 8 * u:8 * u + 8]))
 
-        nc.scalar.copy(w_p[:].rearrange("p (t m) -> p m t", t=4), w_raw[:].rearrange("p (m t) -> p m t", t=4))
-        nc.scalar.copy(w0_p[:].rearrange("p (t m) -> p m t", t=4), w0_raw[:].rearrange("p (m t) -> p m t", t=4))
+        nc.scalar.copy(w_p[:].rearrange("p (t c i) -> p c t i", t=4, i=4), w_raw[:].rearrange("p (c i t) -> p c t i", t=4, i=4))
+        nc.scalar.copy(w0_p[:].rearrange("p (t c i) -> p c t i", t=4, i=4), w0_raw[:].rearrange("p (c i t) -> p c t i", t=4, i=4))
 
-        a_ps = [psum.tile([P, J], F32, name="a_ps%d" % t) for t in range(4)]
-        for t in range(4):
+        parts = [(0, 0, P), (0, P, J), (1, 0, J), (2, 0, J), (3, 0, J)]
+        a_ps = [psum.tile([P, hi - lo], F32, name="a_ps%d" % i) for i, (t, lo, hi) in enumerate(parts)]
+        for i, (t, lo, hi) in enumerate(parts):
             c = slice(P * t, P * t + P)
-            nc.tensor.matmul_mx(out=a_ps[t][:], lhsT=w_p[:, c].bitcast(E5M2), lhsT_scale=ww_sp[:, c],
-                                rhs=xt_g[:].bitcast(E2M1), rhs_scale=xt_sg[:], start=True, stop=False)
-        for t in range(4):
+            nc.tensor.matmul_mx(out=a_ps[i][:], lhsT=w_p[:, c].bitcast(E5M2), lhsT_scale=ww_sp[:, c],
+                                rhs=xt_g[:, lo:hi].bitcast(E2M1), rhs_scale=xt_sg[:, lo:hi], start=True, stop=False)
+        for i, (t, lo, hi) in enumerate(parts):
             c = slice(P * t, P * t + P)
-            nc.tensor.matmul_mx(out=a_ps[t][:], lhsT=w0_p[:, c].bitcast(E4M3), lhsT_scale=ww_sp[:, R + P * t:R + P * t + P],
-                                rhs=xo_g[:].bitcast(E5M2), rhs_scale=xo_sg[:], start=False, stop=True)
+            nc.tensor.matmul_mx(out=a_ps[i][:], lhsT=w0_p[:, c].bitcast(E4M3), lhsT_scale=ww_sp[:, R + P * t:R + P * t + P],
+                                rhs=xo_g[:, lo:hi].bitcast(E5M2), rhs_scale=xo_sg[:, lo:hi], start=False, stop=True)
 
         a_sb = [sb_tile("a_sb%d" % t, [P, J], F32) for t in range(4)]
-        for t in range(4):
-            nc.vector.tensor_copy(a_sb[t][:], a_ps[t][:])
+        for i, (t, lo, hi) in enumerate(parts):
+            if t == 0:
+                nc.scalar.copy(a_sb[t][:, lo:hi], a_ps[i][:])
+            else:
+                nc.vector.tensor_copy(a_sb[t][:, lo:hi], a_ps[i][:])
 
         nc.vector.tensor_copy(x6_g[:], xt_w[:].indirect(l6[:]))
         nc.vector.tensor_copy(x6_sg[:], xt_s[:].indirect(l6[:]))

@@ -48,7 +48,6 @@ def tile_list_tripleblend_bank_further_plain_kernel(
         ws_w = sb_tile("ws_w", [P, N], U32)
         xt_s = sb_tile("xt_s", [P, T], U8)
         xo_s = sb_tile("xo_s", [P, T], U8)
-        ww_s = sb_tile("ww_s", [P, 2 * R], U8)
         wo_s = sb_tile("wo_s", [P, 2 * N], U8)
         sa_t = sb_tile("sa_t", [P, 4], F32)
         sb_t = sb_tile("sb_t", [P, 4], F32)
@@ -57,34 +56,36 @@ def tile_list_tripleblend_bank_further_plain_kernel(
         def words(dram):
             return dram[0].rearrange("p n t -> p (n t)").bitcast(I32)
 
+        ww_s_st = sb_tile("ww_s_st", [P, 2, 256], I32)
+        nc.vector.memset(ww_s_st[0:64, :, :], 0)
         nc.vector.memset(xt_s[:].bitcast(I32), 0)
         nc.vector.memset(xo_s[:].bitcast(I32), 0)
-        ww_s_st = sb_tile("ww_s_st", [4, 4, 256], I32)
-        nc.vector.memset(ww_s[:].bitcast(I32), 0)
         nc.vector.memset(wo_s[:].bitcast(I32), 0)
 
-        nc.sync.dma_start(ww_s_st[:, :, 0:128], w_scales[0].bitcast(I32).rearrange("(q r) c -> r q c", r=4))
-        nc.sync.dma_start(ww_s_st[:, :, 128:256], w0_scales[0].bitcast(I32).rearrange("(q r) c -> r q c", r=4))
         nc.sync.dma_start(l1[:], offs)
+        nc.sync.dma_start(l2[:], offs2)
         nc.sync.dma_start(xt_w[:].bitcast(I32), xt_words[0].bitcast(I32))
+        nc.sync.dma_start(ww_s_st[0:4, :, 0:128], w_scales[0].bitcast(I32).rearrange("(b h r) c -> h r b c", b=2, h=2)[0])
+        nc.sync.dma_start(ww_s_st[32:36, :, 0:128], w_scales[0].bitcast(I32).rearrange("(b h r) c -> h r b c", b=2, h=2)[1])
+        nc.sync.dma_start(ww_s_st[0:4, :, 128:256], w0_scales[0].bitcast(I32).rearrange("(b h r) c -> h r b c", b=2, h=2)[0])
+        nc.sync.dma_start(ww_s_st[32:36, :, 128:256], w0_scales[0].bitcast(I32).rearrange("(b h r) c -> h r b c", b=2, h=2)[1])
+        nc.sync.dma_start(xo_w[:].bitcast(I32), words(xo_words))
+        nc.gpsimd.dma_start(w_raw[:].bitcast(I32), words(w_words))
+        nc.gpsimd.dma_start(w0_raw[:].bitcast(I32), words(w0_words))
+        nc.gpsimd.dma_start(xo_s[96:100, :].bitcast(I32)[:, 0:256], xo_scales[0].bitcast(I32)[12:16, :])
         nc.sync.dma_start(xt_s[0:4, :].bitcast(I32)[:, 0:256], xt_scales[0].bitcast(I32)[0:4, :])
         nc.sync.dma_start(xt_s[32:36, :].bitcast(I32)[:, 0:256], xt_scales[0].bitcast(I32)[4:8, :])
-        nc.sync.dma_start(w_raw[:].bitcast(I32), words(w_words))
-        nc.sync.dma_start(xo_w[:].bitcast(I32), words(xo_words))
-        nc.gpsimd.dma_start(sa_t[:], sa.rearrange("(p t) o -> p (t o)", t=4))
-        nc.gpsimd.dma_start(sb_t[:], sb.rearrange("(p t) o -> p (t o)", t=4))
-        nc.gpsimd.dma_start(sd_t[:], sd.rearrange("(p t) o -> p (t o)", t=4))
         nc.sync.dma_start(xt_s[64:68, :].bitcast(I32)[:, 0:256], xt_scales[0].bitcast(I32)[8:12, :])
         nc.sync.dma_start(xt_s[96:100, :].bitcast(I32)[:, 0:256], xt_scales[0].bitcast(I32)[12:16, :])
-        nc.sync.dma_start(l2[:], offs2)
-        nc.sync.dma_start(w0_raw[:].bitcast(I32), words(w0_words))
         nc.sync.dma_start(xo_s[0:4, :].bitcast(I32)[:, 0:256], xo_scales[0].bitcast(I32)[0:4, :])
         nc.sync.dma_start(xo_s[32:36, :].bitcast(I32)[:, 0:256], xo_scales[0].bitcast(I32)[4:8, :])
         nc.sync.dma_start(xo_s[64:68, :].bitcast(I32)[:, 0:256], xo_scales[0].bitcast(I32)[8:12, :])
-        nc.sync.dma_start(xo_s[96:100, :].bitcast(I32)[:, 0:256], xo_scales[0].bitcast(I32)[12:16, :])
         nc.sync.dma_start(l3[:], offs3)
+        nc.sync.dma_start(sa_t[:], sa.rearrange("(p t) o -> p (t o)", t=4))
         nc.sync.dma_start(l4[:], offs4)
+        nc.sync.dma_start(sb_t[:], sb.rearrange("(p t) o -> p (t o)", t=4))
         nc.sync.dma_start(l5[:], offs5)
+        nc.sync.dma_start(sd_t[:], sd.rearrange("(p t) o -> p (t o)", t=4))
         nc.sync.dma_start(l6[:], offs6)
         nc.sync.dma_start(ws_w[:].bitcast(I32), words(ws_words))
         nc.sync.dma_start(wb_w[:].bitcast(I32), words(wb_words))
@@ -104,15 +105,14 @@ def tile_list_tripleblend_bank_further_plain_kernel(
         xt_sg = sb_tile("xt_sg", [P, J], U8)
         xo_g = sb_tile("xo_g", [P, J], U32)
         xo_sg = sb_tile("xo_sg", [P, J], U8)
-        x6_g = sb_tile("x6_g", [P, O], U16, "xo_s")
+        x6_g = sb_tile("x6_g", [P, O], U16, "w0_p")
         x6_sg = sb_tile("x6_sg", [P, O], U8, "xo_g")
 
-        for q in range(4):
-            nc.vector.tensor_copy(ww_s[32 * q:32 * q + 4, :].bitcast(I32), ww_s_st[:, q, :])
-        nc.vector.tensor_copy(ww_sp[:].rearrange("p (a t m) -> p a t m", a=2, t=4), ww_s[:].rearrange("p (a m t) -> p a t m", a=2, t=4))
         nc.vector.tensor_copy(xt_g[:], xt_w[:].indirect(l1[:]))
-        nc.vector.tensor_copy(xt_sg[:], xt_s[:].indirect(l1[:]))
+        nc.vector.tensor_copy(ww_s_st[64:128, 0, :], ww_s_st[0:64, 1, :])
+        nc.vector.tensor_copy(ww_sp[:].rearrange("p (a t m) -> p a t m", a=2, t=4), ww_s_st[:, 0, :].bitcast(U8).rearrange("p (a m t) -> p a t m", a=2, t=4))
         nc.vector.tensor_copy(xo_g[:], xo_w[:].indirect(l2[:]))
+        nc.vector.tensor_copy(xt_sg[:], xt_s[:].indirect(l1[:]))
         for u in range(2):
             nc.vector.tensor_copy(xo_sg[:, P * u:P * u + P], xo_s[:].indirect(l2[:, 8 * u:8 * u + 8]))
 
@@ -121,14 +121,15 @@ def tile_list_tripleblend_bank_further_plain_kernel(
 
         parts = [(0, 0, P), (0, P, J), (1, 0, J), (2, 0, J), (3, 0, J)]
         a_ps = [psum.tile([P, hi - lo], F32, name="a_ps%d" % i) for i, (t, lo, hi) in enumerate(parts)]
-        for i, (t, lo, hi) in enumerate(parts):
+        for t in range(4):
             c = slice(P * t, P * t + P)
-            nc.tensor.matmul_mx(out=a_ps[i][:], lhsT=w_p[:, c].bitcast(E5M2), lhsT_scale=ww_sp[:, c],
-                                rhs=xt_g[:, lo:hi].bitcast(E2M1), rhs_scale=xt_sg[:, lo:hi], start=True, stop=False)
-        for i, (t, lo, hi) in enumerate(parts):
-            c = slice(P * t, P * t + P)
-            nc.tensor.matmul_mx(out=a_ps[i][:], lhsT=w0_p[:, c].bitcast(E4M3), lhsT_scale=ww_sp[:, R + P * t:R + P * t + P],
-                                rhs=xo_g[:, lo:hi].bitcast(E5M2), rhs_scale=xo_sg[:, lo:hi], start=False, stop=True)
+            mine = [(i, lo, hi) for i, (u, lo, hi) in enumerate(parts) if u == t]
+            for i, lo, hi in mine:
+                nc.tensor.matmul_mx(out=a_ps[i][:], lhsT=w_p[:, c].bitcast(E5M2), lhsT_scale=ww_sp[:, c],
+                                    rhs=xt_g[:, lo:hi].bitcast(E2M1), rhs_scale=xt_sg[:, lo:hi], start=True, stop=False)
+            for i, lo, hi in mine:
+                nc.tensor.matmul_mx(out=a_ps[i][:], lhsT=w0_p[:, c].bitcast(E4M3), lhsT_scale=ww_sp[:, R + P * t:R + P * t + P],
+                                    rhs=xo_g[:, lo:hi].bitcast(E5M2), rhs_scale=xo_sg[:, lo:hi], start=False, stop=True)
 
         a_sb = [sb_tile("a_sb%d" % t, [P, J], F32) for t in range(4)]
         for i, (t, lo, hi) in enumerate(parts):

from contextlib import ExitStack

import concourse.mybir as mybir

F32 = mybir.dt.float32
BF16 = mybir.dt.bfloat16
I32 = mybir.dt.int32
U32 = mybir.dt.uint32
U16 = mybir.dt.uint16
U8 = mybir.dt.uint8
E4M3 = mybir.dt.float8_e4m3fn_x4
E5M2 = mybir.dt.float8_e5m2_x4
E2M1 = mybir.dt.float4_e2m1fn_x4
ALU = mybir.AluOpType
ACT = mybir.ActivationFunctionType

P = 128
T, J, R, O, N = 1024, 256, 512, 128, 256
FLOPS = 335544320


def tile_list_tripleblend_bank_further_plain_kernel(
    tc, xt_words, xt_scales, w_words, w_scales, xo_words, xo_scales, w0_words, w0_scales,
    sa, sb, sd, wb_words, wb_scales, ws_words, ws_scales,
    offs, offs2, offs3, offs4, offs5, offs6, out,
):
    nc = tc.nc
    with ExitStack() as ctx:
        lists = ctx.enter_context(tc.tile_pool(name="lists", bufs=1))
        keep = ctx.enter_context(tc.tile_pool(name="keep", bufs=1))
        psum = ctx.enter_context(tc.psum_pool(name="psum", bufs=1))

        def sb_tile(name, shape, dtype, tag=None):
            return keep.tile(shape, dtype, name=name, tag=tag or name, align_bytes=64)

        l1 = lists.tile([P, J // 16], U16, name="l1")
        l2 = lists.tile([P, J // 16], U16, name="l2")
        l3 = lists.tile([P, O // 16], U16, name="l3")
        l4 = lists.tile([P, O // 16], U16, name="l4")
        l5 = lists.tile([P, O // 16], U16, name="l5")
        l6 = lists.tile([P, O // 16], U16, name="l6")

        xt_w = sb_tile("xt_w", [P, T], U16)
        xo_w = sb_tile("xo_w", [P, T], U32)
        w_raw = sb_tile("w_raw", [P, R], U32)
        w0_raw = sb_tile("w0_raw", [P, R], U32)
        wb_w = sb_tile("wb_w", [P, N], U32)
        ws_w = sb_tile("ws_w", [P, N], U32)
        xt_s = sb_tile("xt_s", [P, T], U8)
        xo_s = sb_tile("xo_s", [P, T], U8)
        wo_s = sb_tile("wo_s", [P, 2 * N], U8)
        sa_t = sb_tile("sa_t", [P, 4], F32)
        sb_t = sb_tile("sb_t", [P, 4], F32)
        sd_t = sb_tile("sd_t", [P, 4], F32)

        def words(dram):
            return dram[0].rearrange("p n t -> p (n t)").bitcast(I32)

        ww_s_st = sb_tile("ww_s_st", [P, 2, 256], I32)
        nc.vector.memset(ww_s_st[0:64, :, :], 0)
        nc.vector.memset(xt_s[:].bitcast(I32), 0)
        nc.vector.memset(xo_s[:].bitcast(I32), 0)
        nc.vector.memset(wo_s[:].bitcast(I32), 0)

        nc.sync.dma_start(l1[:], offs)
        nc.sync.dma_start(l2[:], offs2)
        nc.sync.dma_start(xt_w[:].bitcast(I32), xt_words[0].bitcast(I32))
        nc.sync.dma_start(ww_s_st[0:4, :, 0:128], w_scales[0].bitcast(I32).rearrange("(b h r) c -> h r b c", b=2, h=2)[0])
        nc.sync.dma_start(ww_s_st[32:36, :, 0:128], w_scales[0].bitcast(I32).rearrange("(b h r) c -> h r b c", b=2, h=2)[1])
        nc.sync.dma_start(ww_s_st[0:4, :, 128:256], w0_scales[0].bitcast(I32).rearrange("(b h r) c -> h r b c", b=2, h=2)[0])
        nc.sync.dma_start(ww_s_st[32:36, :, 128:256], w0_scales[0].bitcast(I32).rearrange("(b h r) c -> h r b c", b=2, h=2)[1])
        nc.sync.dma_start(xo_w[:].bitcast(I32), words(xo_words))
        nc.gpsimd.dma_start(w_raw[:].bitcast(I32), words(w_words))
        nc.gpsimd.dma_start(w0_raw[:].bitcast(I32), words(w0_words))
        nc.gpsimd.dma_start(xo_s[96:100, :].bitcast(I32)[:, 0:256], xo_scales[0].bitcast(I32)[12:16, :])
        nc.sync.dma_start(xt_s[0:4, :].bitcast(I32)[:, 0:256], xt_scales[0].bitcast(I32)[0:4, :])
        nc.sync.dma_start(xt_s[32:36, :].bitcast(I32)[:, 0:256], xt_scales[0].bitcast(I32)[4:8, :])
        nc.sync.dma_start(xt_s[64:68, :].bitcast(I32)[:, 0:256], xt_scales[0].bitcast(I32)[8:12, :])
        nc.sync.dma_start(xt_s[96:100, :].bitcast(I32)[:, 0:256], xt_scales[0].bitcast(I32)[12:16, :])
        nc.sync.dma_start(xo_s[0:4, :].bitcast(I32)[:, 0:256], xo_scales[0].bitcast(I32)[0:4, :])
        nc.sync.dma_start(xo_s[32:36, :].bitcast(I32)[:, 0:256], xo_scales[0].bitcast(I32)[4:8, :])
        nc.sync.dma_start(xo_s[64:68, :].bitcast(I32)[:, 0:256], xo_scales[0].bitcast(I32)[8:12, :])
        nc.sync.dma_start(l3[:], offs3)
        nc.sync.dma_start(sa_t[:], sa.rearrange("(p t) o -> p (t o)", t=4))
        nc.sync.dma_start(l4[:], offs4)
        nc.sync.dma_start(sb_t[:], sb.rearrange("(p t) o -> p (t o)", t=4))
        nc.sync.dma_start(l5[:], offs5)
        nc.sync.dma_start(sd_t[:], sd.rearrange("(p t) o -> p (t o)", t=4))
        nc.sync.dma_start(l6[:], offs6)
        nc.sync.dma_start(ws_w[:].bitcast(I32), words(ws_words))
        nc.sync.dma_start(wb_w[:].bitcast(I32), words(wb_words))
        nc.sync.dma_start(wo_s[0:4, :].bitcast(I32)[:, 64:128], ws_scales[0].bitcast(I32)[0:4, :])
        nc.sync.dma_start(wo_s[32:36, :].bitcast(I32)[:, 64:128], ws_scales[0].bitcast(I32)[4:8, :])
        nc.sync.dma_start(wo_s[64:68, :].bitcast(I32)[:, 64:128], ws_scales[0].bitcast(I32)[8:12, :])
        nc.sync.dma_start(wo_s[96:100, :].bitcast(I32)[:, 64:128], ws_scales[0].bitcast(I32)[12:16, :])
        nc.sync.dma_start(wo_s[0:4, :].bitcast(I32)[:, 0:64], wb_scales[0].bitcast(I32)[0:4, :])
        nc.sync.dma_start(wo_s[32:36, :].bitcast(I32)[:, 0:64], wb_scales[0].bitcast(I32)[4:8, :])
        nc.sync.dma_start(wo_s[64:68, :].bitcast(I32)[:, 0:64], wb_scales[0].bitcast(I32)[8:12, :])
        nc.sync.dma_start(wo_s[96:100, :].bitcast(I32)[:, 0:64], wb_scales[0].bitcast(I32)[12:16, :])

        w_p = sb_tile("w_p", [P, R], U32)
        w0_p = sb_tile("w0_p", [P, R], U32)
        ww_sp = sb_tile("ww_sp", [P, 2 * R], U8)
        xt_g = sb_tile("xt_g", [P, J], U16)
        xt_sg = sb_tile("xt_sg", [P, J], U8)
        xo_g = sb_tile("xo_g", [P, J], U32)
        xo_sg = sb_tile("xo_sg", [P, J], U8)
        x6_g = sb_tile("x6_g", [P, O], U16, "w0_p")
        x6_sg = sb_tile("x6_sg", [P, O], U8, "xo_g")

        nc.vector.tensor_copy(xt_g[:], xt_w[:].indirect(l1[:]))
        nc.vector.tensor_copy(ww_s_st[64:128, 0, :], ww_s_st[0:64, 1, :])
        nc.vector.tensor_copy(ww_sp[:].rearrange("p (a t m) -> p a t m", a=2, t=4), ww_s_st[:, 0, :].bitcast(U8).rearrange("p (a m t) -> p a t m", a=2, t=4))
        nc.vector.tensor_copy(xo_g[:], xo_w[:].indirect(l2[:]))
        nc.vector.tensor_copy(xt_sg[:], xt_s[:].indirect(l1[:]))
        for u in range(2):
            nc.vector.tensor_copy(xo_sg[:, P * u:P * u + P], xo_s[:].indirect(l2[:, 8 * u:8 * u + 8]))

        nc.scalar.copy(w_p[:].rearrange("p (t c i) -> p c t i", t=4, i=4), w_raw[:].rearrange("p (c i t) -> p c t i", t=4, i=4))
        nc.scalar.copy(w0_p[:].rearrange("p (t c i) -> p c t i", t=4, i=4), w0_raw[:].rearrange("p (c i t) -> p c t i", t=4, i=4))

        parts = [(0, 0, P), (0, P, J), (1, 0, J), (2, 0, J), (3, 0, J)]
        a_ps = [psum.tile([P, hi - lo], F32, name="a_ps%d" % i) for i, (t, lo, hi) in enumerate(parts)]
        for t in range(4):
            c = slice(P * t, P * t + P)
            mine = [(i, lo, hi) for i, (u, lo, hi) in enumerate(parts) if u == t]
            for i, lo, hi in mine:
                nc.tensor.matmul_mx(out=a_ps[i][:], lhsT=w_p[:, c].bitcast(E5M2), lhsT_scale=ww_sp[:, c],
                                    rhs=xt_g[:, lo:hi].bitcast(E2M1), rhs_scale=xt_sg[:, lo:hi], start=True, stop=False)
            for i, lo, hi in mine:
                nc.tensor.matmul_mx(out=a_ps[i][:], lhsT=w0_p[:, c].bitcast(E4M3), lhsT_scale=ww_sp[:, R + P * t:R + P * t + P],
                                    rhs=xo_g[:, lo:hi].bitcast(E5M2), rhs_scale=xo_sg[:, lo:hi], start=False, stop=True)

        a_sb = [sb_tile("a_sb%d" % t, [P, J], F32) for t in range(4)]
        for i, (t, lo, hi) in enumerate(parts):
            if t == 0:
                nc.scalar.copy(a_sb[t][:, lo:hi], a_ps[i][:])
            else:
                nc.vector.tensor_copy(a_sb[t][:, lo:hi], a_ps[i][:])

        nc.vector.tensor_copy(x6_g[:], xt_w[:].indirect(l6[:]))
        nc.vector.tensor_copy(x6_sg[:], xt_s[:].indirect(l6[:]))
        y_ps = [psum.tile([P, O], F32, name="y_ps%d" % h) for h in range(2)]
        for h in range(2):
            nc.tensor.matmul_mx(out=y_ps[h][:], lhsT=ws_w[:, P * h:P * h + P].bitcast(E4M3), lhsT_scale=wo_s[:, N + P * h:N + P * h + P],
                                rhs=x6_g[:].bitcast(E2M1), rhs_scale=x6_sg[:], start=True, stop=False)

        ga = sb_tile("ga", [P, 4, O], F32)
        gb = sb_tile("gb", [P, 4, O], F32)
        gd = sb_tile("gd", [P, 4, O], F32)
        s2 = sb_tile("s2", [P, 4, O], F32, "xt_w")
        s3 = sb_tile("s3", [P, 4, O], F32, "xt_s")
        hb = sb_tile("hb", [P, O, 4], BF16)
        hq = sb_tile("hq", [P, O], U32)
        hs = sb_tile("hs", [P, O], U8)

        def blend(t, lo, hi):
            c = slice(lo, hi)
            k = slice(lo // 16, hi // 16)
            nc.scalar.activation(ga[:, t, c], a_sb[t][:].indirect(l3[:, k]), ACT.Copy, scale=sa_t[:, t:t + 1])
            nc.scalar.activation(gb[:, t, c], a_sb[t][:].indirect(l4[:, k]), ACT.Copy, scale=sb_t[:, t:t + 1])
            nc.vector.tensor_tensor(s2[:, t, c], ga[:, t, c], gb[:, t, c], ALU.add)
            nc.scalar.activation(gd[:, t, c], a_sb[t][:].indirect(l5[:, k]), ACT.Copy, scale=sd_t[:, t:t + 1])
            nc.vector.tensor_tensor(s3[:, t, c], s2[:, t, c], gd[:, t, c], ALU.add)

        for t in range(3):
            blend(t, 0, O)
        for lo in (0, O // 2):
            hi = lo + O // 2
            blend(3, lo, hi)
            nc.vector.tensor_scalar(hb[:, lo:hi, :], s3[:, :, lo:hi].rearrange("p t o -> p o t"), 0.0, None, ALU.max)
            nc.vector.quantize_mx(out=hq[:, lo:hi].bitcast(E5M2), scales=hs[:, lo:hi], in_=hb[:, lo:hi, :].rearrange("p o t -> p (o t)"))

        for h in range(2):
            nc.tensor.matmul_mx(out=y_ps[h][:], lhsT=wb_w[:, P * h:P * h + P].bitcast(E4M3), lhsT_scale=wo_s[:, P * h:P * h + P],
                                rhs=hq[:].bitcast(E5M2), rhs_scale=hs[:], start=False, stop=True)
        y0 = sb_tile("y0", [P, O], F32)
        y1 = sb_tile("y1", [P, O], F32)
        nc.vector.tensor_copy(y0[:], y_ps[0][:])
        nc.scalar.copy(y1[:], y_ps[1][:])
        nc.sync.dma_start(out[0:P, :], y0[:])
        nc.scalar.dma_start(out[P:2 * P, :], y1[:])
